import numpy as np
import ml_dtypes

BF16 = ml_dtypes.bfloat16


def bf(x):
    return np.asarray(x, np.float32).astype(BF16)


def f32(x):
    return np.asarray(x, np.float32)


def f64(x):
    return np.asarray(x).astype(np.float64)


def striped(idx):
    return np.tile(idx.reshape(-1, 16).T, (8, 1))


S, K, M, N, E, Q = 2048, 128, 256, 4096, 4, 1024


def two_experts():
    first = np.random.permutation(S).reshape(E, S // E)
    return np.concatenate([np.random.permutation(np.concatenate([first[e], first[(e + 1) % E]])) for e in range(E)])


def setup_inputs():
    return {"table": bf(np.random.standard_normal((K, S))), "w": bf(np.random.standard_normal((E, K, M)) / np.sqrt(K)), "c": f32(0.2 + 0.8 * np.random.random_sample((1, N))), "offs": striped(two_experts())}


def reference(table, w, c, offs):
    idx = offs[:16].T.reshape(-1)
    x = f64(table)[:, idx]
    y = np.concatenate([f64(w)[e].T @ x[:, e * Q : (e + 1) * Q] for e in range(E)], axis=1)
    return y * f64(c)

@@ -1,0 +1,51 @@
+import concourse.mybir as mybir
+
+BF16 = mybir.dt.bfloat16
+F32 = mybir.dt.float32
+U16 = mybir.dt.uint16
+
+P = 128
+TOKENS = 2048
+EXPERTS = 4
+M = 256
+N = 4096
+PER_EXPERT = N // EXPERTS
+PIECE = 512
+PIECES = N // PIECE
+HALVES = M // P
+
+FLOPS = 2 * P * M * N
+
+
+def tile_gather_matmul_kernel(tc, table, w, c, offs, out):
+    nc = tc.nc
+    with (
+        tc.tile_pool(name="held", bufs=1) as held,
+        tc.tile_pool(name="ring", bufs=4) as ring,
+        tc.psum_pool(name="banks", bufs=8) as banks,
+    ):
+        offsets = held.tile([P, N // 16], U16, name="offsets")
+        nc.sync.dma_start(offsets[:], offs)
+        tokens = held.tile([P, TOKENS], BF16, name="tokens")
+        nc.scalar.dma_start(tokens[:], table)
+        weights = held.tile([P, EXPERTS, M], BF16, name="weights")
+        nc.sync.dma_start(weights[:], w.rearrange("e k m -> k e m"))
+
+        c_row = c.rearrange("o n -> (o n)")
+        gates = []
+        for piece in range(PIECES):
+            gate = held.tile([P, PIECE], F32, name=f"gate{piece}")
+            queue = nc.sync if piece % 2 == 0 else nc.scalar
+            queue.dma_start(gate[:], c_row[piece * PIECE : (piece + 1) * PIECE].partition_broadcast(P))
+            gates.append(gate)
+
+        for piece in range(PIECES):
+            expert = piece * PIECE // PER_EXPERT
+            picked = tokens[:].indirect(offsets[:, piece * (PIECE // 16) : (piece + 1) * (PIECE // 16)])
+            for half in range(HALVES):
+                bank = banks.tile([P, PIECE], F32, name="bank")
+                nc.tensor.matmul(bank[:], weights[:, expert, half * P : (half + 1) * P], picked, start=True, stop=True)
+                scaled = ring.tile([P, PIECE], F32, name="scaled")
+                nc.vector.tensor_tensor(scaled[:], bank[:], gates[piece][:], mybir.AluOpType.mult)
+                queue = nc.sync if half == 0 else nc.scalar
+                queue.dma_start(out[half * P : (half + 1) * P, piece * PIECE : (piece + 1) * PIECE], scaled[:])

@@ -21,31 +21,33 @@ def tile_gather_matmul_kernel(tc, table, w, c, offs, out):
     nc = tc.nc
     with (
         tc.tile_pool(name="held", bufs=1) as held,
-        tc.tile_pool(name="ring", bufs=4) as ring,
         tc.psum_pool(name="banks", bufs=8) as banks,
     ):
         offsets = held.tile([P, N // 16], U16, name="offsets")
         nc.sync.dma_start(offsets[:], offs)
-        tokens = held.tile([P, TOKENS], BF16, name="tokens")
-        nc.scalar.dma_start(tokens[:], table)
         weights = held.tile([P, EXPERTS, M], BF16, name="weights")
-        nc.sync.dma_start(weights[:], w.rearrange("e k m -> k e m"))
+        nc.scalar.dma_start(weights[:, 0, :], w[0])
+        tokens = held.tile([P, TOKENS], BF16, name="tokens")
+        nc.sync.dma_start(tokens[:, : TOKENS // 2], table[:, : TOKENS // 2])
+        nc.scalar.dma_start(tokens[:, TOKENS // 2 :], table[:, TOKENS // 2 :])
 
         c_row = c.rearrange("o n -> (o n)")
-        gates = []
+        gates = held.tile([P, N], F32, name="gates")
         for piece in range(PIECES):
-            gate = held.tile([P, PIECE], F32, name=f"gate{piece}")
+            entries = slice(piece * PIECE, (piece + 1) * PIECE)
             queue = nc.sync if piece % 2 == 0 else nc.scalar
-            queue.dma_start(gate[:], c_row[piece * PIECE : (piece + 1) * PIECE].partition_broadcast(P))
-            gates.append(gate)
+            queue.dma_start(gates[:, entries], c_row[entries].partition_broadcast(P))
+            if piece < EXPERTS - 1:
+                queue.dma_start(weights[:, piece + 1, :], w[piece + 1])
 
+        staged = held.tile([P, HALVES, N], F32, name="staged")
         for piece in range(PIECES):
+            entries = slice(piece * PIECE, (piece + 1) * PIECE)
             expert = piece * PIECE // PER_EXPERT
             picked = tokens[:].indirect(offsets[:, piece * (PIECE // 16) : (piece + 1) * (PIECE // 16)])
             for half in range(HALVES):
                 bank = banks.tile([P, PIECE], F32, name="bank")
                 nc.tensor.matmul(bank[:], weights[:, expert, half * P : (half + 1) * P], picked, start=True, stop=True)
-                scaled = ring.tile([P, PIECE], F32, name="scaled")
-                nc.vector.tensor_tensor(scaled[:], bank[:], gates[piece][:], mybir.AluOpType.mult)
+                nc.vector.tensor_tensor(staged[:, half, entries], bank[:], gates[:, entries], mybir.AluOpType.mult)
                 queue = nc.sync if half == 0 else nc.scalar
-                queue.dma_start(out[half * P : (half + 1) * P, piece * PIECE : (piece + 1) * PIECE], scaled[:])
+                queue.dma_start(out[half * P : (half + 1) * P, entries], staged[:, half, entries])

@@ -14,6 +14,8 @@ PIECE = 512
 PIECES = N // PIECE
 HALVES = M // P
 
+WARM_UP = 8
+
 FLOPS = 2 * P * M * N
 
 
@@ -21,8 +23,15 @@ def tile_gather_matmul_kernel(tc, table, w, c, offs, out):
     nc = tc.nc
     with (
         tc.tile_pool(name="held", bufs=1) as held,
-        tc.psum_pool(name="banks", bufs=8) as banks,
+        tc.psum_pool(name="idle", bufs=1) as idle,
+        tc.psum_pool(name="banks", bufs=7) as banks,
     ):
+        zeros = held.tile([P, PIECE], BF16, name="zeros")
+        nc.vector.memset(zeros[:], 0.0)
+        unused = idle.tile([P, PIECE], F32, name="unused")
+        for warm in range(WARM_UP):
+            nc.tensor.matmul(unused[:], zeros[:, :P], zeros[:], start=True, stop=True)
+
         offsets = held.tile([P, N // 16], U16, name="offsets")
         nc.sync.dma_start(offsets[:], offs)
         weights = held.tile([P, EXPERTS, M], BF16, name="weights")

@@ -11,52 +11,50 @@ M = 256
 N = 4096
 PER_EXPERT = N // EXPERTS
 PIECE = 512
-PIECES = N // PIECE
+PIECES_PER_EXPERT = PER_EXPERT // PIECE
 HALVES = M // P
-
-WARM_UP = 8
 
 FLOPS = 2 * P * M * N
 
 
 def tile_gather_matmul_kernel(tc, table, w, c, offs, out):
     nc = tc.nc
+    mult = mybir.AluOpType.mult
     with (
         tc.tile_pool(name="held", bufs=1) as held,
-        tc.psum_pool(name="idle", bufs=1) as idle,
-        tc.psum_pool(name="banks", bufs=7) as banks,
+        tc.psum_pool(name="banks", bufs=8) as banks,
     ):
-        zeros = held.tile([P, PIECE], BF16, name="zeros")
-        nc.vector.memset(zeros[:], 0.0)
-        unused = idle.tile([P, PIECE], F32, name="unused")
-        for warm in range(WARM_UP):
-            nc.tensor.matmul(unused[:], zeros[:, :P], zeros[:], start=True, stop=True)
-
         offsets = held.tile([P, N // 16], U16, name="offsets")
         nc.sync.dma_start(offsets[:], offs)
         weights = held.tile([P, EXPERTS, M], BF16, name="weights")
-        nc.scalar.dma_start(weights[:, 0, :], w[0])
+        nc.sync.dma_start(weights[:, 0, :], w[0])
         tokens = held.tile([P, TOKENS], BF16, name="tokens")
-        nc.sync.dma_start(tokens[:, : TOKENS // 2], table[:, : TOKENS // 2])
-        nc.scalar.dma_start(tokens[:, TOKENS // 2 :], table[:, TOKENS // 2 :])
+        nc.scalar.dma_start(tokens[:], table)
 
         c_row = c.rearrange("o n -> (o n)")
         gates = held.tile([P, N], F32, name="gates")
-        for piece in range(PIECES):
-            entries = slice(piece * PIECE, (piece + 1) * PIECE)
-            queue = nc.sync if piece % 2 == 0 else nc.scalar
+        for expert in range(EXPERTS):
+            entries = slice(expert * PER_EXPERT, (expert + 1) * PER_EXPERT)
+            queue = nc.sync if expert % 2 == 0 else nc.scalar
             queue.dma_start(gates[:, entries], c_row[entries].partition_broadcast(P))
-            if piece < EXPERTS - 1:
-                queue.dma_start(weights[:, piece + 1, :], w[piece + 1])
+            if expert + 1 < EXPERTS:
+                queue.dma_start(weights[:, expert + 1, :], w[expert + 1])
 
         staged = held.tile([P, HALVES, N], F32, name="staged")
-        for piece in range(PIECES):
-            entries = slice(piece * PIECE, (piece + 1) * PIECE)
-            expert = piece * PIECE // PER_EXPERT
-            picked = tokens[:].indirect(offsets[:, piece * (PIECE // 16) : (piece + 1) * (PIECE // 16)])
+        for expert in range(EXPERTS):
+            last_expert = expert == EXPERTS - 1
             for half in range(HALVES):
-                bank = banks.tile([P, PIECE], F32, name="bank")
-                nc.tensor.matmul(bank[:], weights[:, expert, half * P : (half + 1) * P], picked, start=True, stop=True)
-                nc.vector.tensor_tensor(staged[:, half, entries], bank[:], gates[:, entries], mybir.AluOpType.mult)
+                rows = slice(half * P, (half + 1) * P)
                 queue = nc.sync if half == 0 else nc.scalar
-                queue.dma_start(out[half * P : (half + 1) * P, entries], staged[:, half, entries])
+                for piece in range(PIECES_PER_EXPERT):
+                    first = expert * PER_EXPERT + piece * PIECE
+                    entries = slice(first, first + PIECE)
+                    picked = tokens[:].indirect(offsets[:, first // 16 : (first + PIECE) // 16])
+                    bank = banks.tile([P, PIECE], F32, name="bank")
+                    nc.tensor.matmul(bank[:], weights[:, expert, rows], picked, start=True, stop=True)
+                    nc.vector.tensor_tensor(staged[:, half, entries], bank[:], gates[:, entries], mult)
+                    if last_expert:
+                        queue.dma_start(out[rows, entries], staged[:, half, entries])
+                if not last_expert:
+                    entries = slice(expert * PER_EXPERT, (expert + 1) * PER_EXPERT)
+                    queue.dma_start(out[rows, entries], staged[:, half, entries])

@@ -1,4 +1,5 @@
 import concourse.mybir as mybir
+from concourse.masks import make_identity
 
 BF16 = mybir.dt.bfloat16
 F32 = mybir.dt.float32
@@ -26,26 +27,42 @@ def tile_gather_matmul_kernel(tc, table, w, c, offs, out):
     ):
         offsets = held.tile([P, N // 16], U16, name="offsets")
         nc.sync.dma_start(offsets[:], offs)
+        c_rows = held.tile([P, P], F32, name="c_rows")
+        nc.scalar.dma_start(c_rows[: N // P, :], c.rearrange("o (b p) -> (o b) p", p=P))
+        nc.vector.memset(c_rows[32:64, :], 0.0)
+        nc.vector.memset(c_rows[64:, :], 0.0)
         weights = held.tile([P, EXPERTS, M], BF16, name="weights")
-        nc.sync.dma_start(weights[:, 0, :], w[0])
+        nc.scalar.dma_start(weights[:, 0, :], w[0])
         tokens = held.tile([P, TOKENS], BF16, name="tokens")
-        nc.scalar.dma_start(tokens[:], table)
+        nc.sync.dma_start(tokens[:, : TOKENS // 2], table[:, : TOKENS // 2])
+        nc.scalar.dma_start(tokens[:, TOKENS // 2 :], table[:, TOKENS // 2 :])
+        nc.sync.dma_start(weights[:, 1:, :], w[1:].rearrange("e k m -> k e m"))
 
         c_row = c.rearrange("o n -> (o n)")
         gates = held.tile([P, N], F32, name="gates")
-        for expert in range(EXPERTS):
+        for expert in range(1, EXPERTS):
             entries = slice(expert * PER_EXPERT, (expert + 1) * PER_EXPERT)
             queue = nc.sync if expert % 2 == 0 else nc.scalar
             queue.dma_start(gates[:, entries], c_row[entries].partition_broadcast(P))
-            if expert + 1 < EXPERTS:
-                queue.dma_start(weights[:, expert + 1, :], w[expert + 1])
+
+        identity = held.tile([P, P], F32, name="identity")
+        make_identity(nc, identity[:])
+        flipped = banks.tile([P, PIECE], F32, name="bank")
+        nc.tensor.transpose(flipped[:, :P], c_rows[:], identity[:])
+        c_cols = held.tile([P, PER_EXPERT // P], F32, name="c_cols")
+        nc.vector.tensor_copy(c_cols[:], flipped[:, : PER_EXPERT // P])
+        for piece in range(PIECES_PER_EXPERT):
+            spread = banks.tile([P, PIECE], F32, name="bank")
+            for q in range(PIECE // P):
+                b = piece * (PIECE // P) + q
+                nc.tensor.transpose(spread[:, q * P : (q + 1) * P], c_cols[:, b : b + 1].to_broadcast([P, P]), identity[:])
+            nc.vector.tensor_copy(gates[:, piece * PIECE : (piece + 1) * PIECE], spread[:])
 
         staged = held.tile([P, HALVES, N], F32, name="staged")
         for expert in range(EXPERTS):
             last_expert = expert == EXPERTS - 1
             for half in range(HALVES):
                 rows = slice(half * P, (half + 1) * P)
-                queue = nc.sync if half == 0 else nc.scalar
                 for piece in range(PIECES_PER_EXPERT):
                     first = expert * PER_EXPERT + piece * PIECE
                     entries = slice(first, first + PIECE)
@@ -54,7 +71,9 @@ def tile_gather_matmul_kernel(tc, table, w, c, offs, out):
                     nc.tensor.matmul(bank[:], weights[:, expert, rows], picked, start=True, stop=True)
                     nc.vector.tensor_tensor(staged[:, half, entries], bank[:], gates[:, entries], mult)
                     if last_expert:
+                        queue = nc.sync if piece == 0 else nc.scalar
                         queue.dma_start(out[rows, entries], staged[:, half, entries])
                 if not last_expert:
                     entries = slice(expert * PER_EXPERT, (expert + 1) * PER_EXPERT)
+                    queue = nc.sync if half == 0 else nc.scalar
                     queue.dma_start(out[rows, entries], staged[:, half, entries])

@@ -40,10 +40,10 @@ def tile_gather_matmul_kernel(tc, table, w, c, offs, out):
 
         c_row = c.rearrange("o n -> (o n)")
         gates = held.tile([P, N], F32, name="gates")
-        for expert in range(1, EXPERTS):
-            entries = slice(expert * PER_EXPERT, (expert + 1) * PER_EXPERT)
-            queue = nc.sync if expert % 2 == 0 else nc.scalar
-            queue.dma_start(gates[:, entries], c_row[entries].partition_broadcast(P))
+        soon = slice(PER_EXPERT, 2 * PER_EXPERT)
+        later = slice(2 * PER_EXPERT, N)
+        nc.scalar.dma_start(gates[:, soon], c_row[soon].partition_broadcast(P))
+        nc.sync.dma_start(gates[:, later], c_row[later].partition_broadcast(P))
 
         identity = held.tile([P, P], F32, name="identity")
         make_identity(nc, identity[:])

@@ -14,6 +14,7 @@ PER_EXPERT = N // EXPERTS
 PIECE = 512
 PIECES_PER_EXPERT = PER_EXPERT // PIECE
 HALVES = M // P
+BLOCKS = PIECE // P
 
 FLOPS = 2 * P * M * N
 
@@ -34,46 +35,45 @@ def tile_gather_matmul_kernel(tc, table, w, c, offs, out):
         weights = held.tile([P, EXPERTS, M], BF16, name="weights")
         nc.scalar.dma_start(weights[:, 0, :], w[0])
         tokens = held.tile([P, TOKENS], BF16, name="tokens")
-        nc.sync.dma_start(tokens[:, : TOKENS // 2], table[:, : TOKENS // 2])
-        nc.scalar.dma_start(tokens[:, TOKENS // 2 :], table[:, TOKENS // 2 :])
+        nc.sync.dma_start(tokens[:], table)
         nc.sync.dma_start(weights[:, 1:, :], w[1:].rearrange("e k m -> k e m"))
 
         c_row = c.rearrange("o n -> (o n)")
         gates = held.tile([P, N], F32, name="gates")
-        soon = slice(PER_EXPERT, 2 * PER_EXPERT)
-        later = slice(2 * PER_EXPERT, N)
-        nc.scalar.dma_start(gates[:, soon], c_row[soon].partition_broadcast(P))
-        nc.sync.dma_start(gates[:, later], c_row[later].partition_broadcast(P))
+        for entries in (slice(PIECE, 2 * PER_EXPERT), slice(2 * PER_EXPERT, N)):
+            nc.sync.dma_start(gates[:, entries], c_row[entries].partition_broadcast(P))
 
         identity = held.tile([P, P], F32, name="identity")
         make_identity(nc, identity[:])
         flipped = banks.tile([P, PIECE], F32, name="bank")
         nc.tensor.transpose(flipped[:, :P], c_rows[:], identity[:])
-        c_cols = held.tile([P, PER_EXPERT // P], F32, name="c_cols")
-        nc.vector.tensor_copy(c_cols[:], flipped[:, : PER_EXPERT // P])
-        for piece in range(PIECES_PER_EXPERT):
-            spread = banks.tile([P, PIECE], F32, name="bank")
-            for q in range(PIECE // P):
-                b = piece * (PIECE // P) + q
-                nc.tensor.transpose(spread[:, q * P : (q + 1) * P], c_cols[:, b : b + 1].to_broadcast([P, P]), identity[:])
-            nc.vector.tensor_copy(gates[:, piece * PIECE : (piece + 1) * PIECE], spread[:])
+        c_cols = held.tile([P, BLOCKS], F32, name="c_cols")
+        nc.vector.tensor_copy(c_cols[:], flipped[:, :BLOCKS])
+        spread = banks.tile([P, PIECE], F32, name="bank")
+        for b in range(BLOCKS):
+            nc.tensor.transpose(spread[:, b * P : (b + 1) * P], c_cols[:, b : b + 1].to_broadcast([P, P]), identity[:])
+        nc.vector.tensor_copy(gates[:, :PIECE], spread[:])
 
         staged = held.tile([P, HALVES, N], F32, name="staged")
         for expert in range(EXPERTS):
-            last_expert = expert == EXPERTS - 1
-            for half in range(HALVES):
+            if expert == 0:
+                products = [(half, piece) for piece in range(PIECES_PER_EXPERT) for half in range(HALVES)]
+            else:
+                products = [(half, piece) for half in range(HALVES) for piece in range(PIECES_PER_EXPERT)]
+            for half, piece in products:
+                first = expert * PER_EXPERT + piece * PIECE
+                entries = slice(first, first + PIECE)
                 rows = slice(half * P, (half + 1) * P)
-                for piece in range(PIECES_PER_EXPERT):
-                    first = expert * PER_EXPERT + piece * PIECE
-                    entries = slice(first, first + PIECE)
-                    picked = tokens[:].indirect(offsets[:, first // 16 : (first + PIECE) // 16])
-                    bank = banks.tile([P, PIECE], F32, name="bank")
-                    nc.tensor.matmul(bank[:], weights[:, expert, rows], picked, start=True, stop=True)
-                    nc.vector.tensor_tensor(staged[:, half, entries], bank[:], gates[:, entries], mult)
-                    if last_expert:
-                        queue = nc.sync if piece == 0 else nc.scalar
-                        queue.dma_start(out[rows, entries], staged[:, half, entries])
-                if not last_expert:
+                picked = tokens[:].indirect(offsets[:, first // 16 : (first + PIECE) // 16])
+                bank = banks.tile([P, PIECE], F32, name="bank")
+                nc.tensor.matmul(bank[:], weights[:, expert, rows], picked, start=True, stop=True)
+                nc.vector.tensor_tensor(staged[:, half, entries], bank[:], gates[:, entries], mult)
+                if expert == 0:
+                    nc.scalar.dma_start(out[rows, entries], staged[:, half, entries])
+                elif expert == EXPERTS - 1:
+                    queue = nc.sync if piece == 0 else nc.scalar
+                    queue.dma_start(out[rows, entries], staged[:, half, entries])
+                elif piece == PIECES_PER_EXPERT - 1:
                     entries = slice(expert * PER_EXPERT, (expert + 1) * PER_EXPERT)
                     queue = nc.sync if half == 0 else nc.scalar
                     queue.dma_start(out[rows, entries], staged[:, half, entries])

@@ -1,5 +1,4 @@
 import concourse.mybir as mybir
-from concourse.masks import make_identity
 
 BF16 = mybir.dt.bfloat16
 F32 = mybir.dt.float32
@@ -14,7 +13,8 @@ PER_EXPERT = N // EXPERTS
 PIECE = 512
 PIECES_PER_EXPERT = PER_EXPERT // PIECE
 HALVES = M // P
-BLOCKS = PIECE // P
+SQUARE = 32
+SQUARES = PIECE // SQUARE
 
 FLOPS = 2 * P * M * N
 
@@ -26,33 +26,33 @@ def tile_gather_matmul_kernel(tc, table, w, c, offs, out):
         tc.tile_pool(name="held", bufs=1) as held,
         tc.psum_pool(name="banks", bufs=8) as banks,
     ):
+        c_row = c.rearrange("o n -> (o n)")
+        c_blocks = held.tile([P, EXPERTS, SQUARE], F32, name="c_blocks", align_bytes=64)
+        for q in range(P // SQUARE):
+            quadrant = slice(q * SQUARE, (q + 1) * SQUARE)
+            nc.sync.dma_start(c_blocks[quadrant, :, :], c_row.rearrange("(e b x) -> b e x", b=SQUARE, x=SQUARE))
         offsets = held.tile([P, N // 16], U16, name="offsets")
         nc.sync.dma_start(offsets[:], offs)
-        c_rows = held.tile([P, P], F32, name="c_rows")
-        nc.scalar.dma_start(c_rows[: N // P, :], c.rearrange("o (b p) -> (o b) p", p=P))
-        nc.vector.memset(c_rows[32:64, :], 0.0)
-        nc.vector.memset(c_rows[64:, :], 0.0)
         weights = held.tile([P, EXPERTS, M], BF16, name="weights")
-        nc.scalar.dma_start(weights[:, 0, :], w[0])
+        nc.sync.dma_start(weights[:, 0, :], w[0])
         tokens = held.tile([P, TOKENS], BF16, name="tokens")
         nc.sync.dma_start(tokens[:], table)
         nc.sync.dma_start(weights[:, 1:, :], w[1:].rearrange("e k m -> k e m"))
 
-        c_row = c.rearrange("o n -> (o n)")
-        gates = held.tile([P, N], F32, name="gates")
-        for entries in (slice(PIECE, 2 * PER_EXPERT), slice(2 * PER_EXPERT, N)):
-            nc.sync.dma_start(gates[:, entries], c_row[entries].partition_broadcast(P))
+        gates = held.tile([P, N], F32, name="gates", align_bytes=64)
+        later = slice(2 * PER_EXPERT, N)
+        nc.sync.dma_start(gates[:, later], c_row[later].partition_broadcast(P))
 
-        identity = held.tile([P, P], F32, name="identity")
-        make_identity(nc, identity[:])
-        flipped = banks.tile([P, PIECE], F32, name="bank")
-        nc.tensor.transpose(flipped[:, :P], c_rows[:], identity[:])
-        c_cols = held.tile([P, BLOCKS], F32, name="c_cols")
-        nc.vector.tensor_copy(c_cols[:], flipped[:, :BLOCKS])
-        spread = banks.tile([P, PIECE], F32, name="bank")
-        for b in range(BLOCKS):
-            nc.tensor.transpose(spread[:, b * P : (b + 1) * P], c_cols[:, b : b + 1].to_broadcast([P, P]), identity[:])
-        nc.vector.tensor_copy(gates[:, :PIECE], spread[:])
+        c_cols = held.tile([P, EXPERTS, SQUARE], F32, name="c_cols", align_bytes=64)
+        nc.vector.transpose(c_cols[:].rearrange("p e b -> p (e b)"), c_blocks[:].rearrange("p e x -> p (e x)"))
+        columns = c_cols[:].rearrange("p e b -> p (e b)")
+        for piece in range(2 * PIECES_PER_EXPERT):
+            wide = held.tile([P, PIECE], F32, name=f"wide{piece}", align_bytes=64)
+            nc.scalar.copy(
+                wide[:].rearrange("p (b x) -> p b x", x=SQUARE),
+                columns[:, piece * SQUARES : (piece + 1) * SQUARES].unsqueeze(2).to_broadcast([P, SQUARES, SQUARE]),
+            )
+            nc.vector.transpose(gates[:, piece * PIECE : (piece + 1) * PIECE], wide[:])
 
         staged = held.tile([P, HALVES, N], F32, name="staged")
         for expert in range(EXPERTS):

import concourse.mybir as mybir

BF16 = mybir.dt.bfloat16
F32 = mybir.dt.float32
U16 = mybir.dt.uint16

P = 128
TOKENS = 2048
EXPERTS = 4
M = 256
N = 4096
PER_EXPERT = N // EXPERTS
PIECE = 512
PIECES_PER_EXPERT = PER_EXPERT // PIECE
HALVES = M // P
SQUARE = 32
SQUARES = PIECE // SQUARE

FLOPS = 2 * P * M * N


def tile_gather_matmul_kernel(tc, table, w, c, offs, out):
    nc = tc.nc
    mult = mybir.AluOpType.mult
    with (
        tc.tile_pool(name="held", bufs=1) as held,
        tc.psum_pool(name="banks", bufs=8) as banks,
    ):
        c_row = c.rearrange("o n -> (o n)")
        c_blocks = held.tile([P, EXPERTS, SQUARE], F32, name="c_blocks", align_bytes=64)
        for q in range(P // SQUARE):
            quadrant = slice(q * SQUARE, (q + 1) * SQUARE)
            nc.sync.dma_start(c_blocks[quadrant, :, :], c_row.rearrange("(e b x) -> b e x", b=SQUARE, x=SQUARE))
        offsets = held.tile([P, N // 16], U16, name="offsets")
        nc.sync.dma_start(offsets[:], offs)
        weights = held.tile([P, EXPERTS, M], BF16, name="weights")
        nc.sync.dma_start(weights[:, 0, :], w[0])
        tokens = held.tile([P, TOKENS], BF16, name="tokens")
        nc.sync.dma_start(tokens[:], table)
        nc.sync.dma_start(weights[:, 1:, :], w[1:].rearrange("e k m -> k e m"))

        gates = held.tile([P, N], F32, name="gates", align_bytes=64)
        later = slice(2 * PER_EXPERT, N)
        nc.sync.dma_start(gates[:, later], c_row[later].partition_broadcast(P))

        c_cols = held.tile([P, EXPERTS, SQUARE], F32, name="c_cols", align_bytes=64)
        nc.vector.transpose(c_cols[:].rearrange("p e b -> p (e b)"), c_blocks[:].rearrange("p e x -> p (e x)"))
        columns = c_cols[:].rearrange("p e b -> p (e b)")
        for piece in range(2 * PIECES_PER_EXPERT):
            wide = held.tile([P, PIECE], F32, name=f"wide{piece}", align_bytes=64)
            nc.scalar.copy(
                wide[:].rearrange("p (b x) -> p b x", x=SQUARE),
                columns[:, piece * SQUARES : (piece + 1) * SQUARES].unsqueeze(2).to_broadcast([P, SQUARES, SQUARE]),
            )
            nc.vector.transpose(gates[:, piece * PIECE : (piece + 1) * PIECE], wide[:])

        staged = held.tile([P, HALVES, N], F32, name="staged")
        for expert in range(EXPERTS):
            if expert == 0:
                products = [(half, piece) for piece in range(PIECES_PER_EXPERT) for half in range(HALVES)]
            else:
                products = [(half, piece) for half in range(HALVES) for piece in range(PIECES_PER_EXPERT)]
            for half, piece in products:
                first = expert * PER_EXPERT + piece * PIECE
                entries = slice(first, first + PIECE)
                rows = slice(half * P, (half + 1) * P)
                picked = tokens[:].indirect(offsets[:, first // 16 : (first + PIECE) // 16])
                bank = banks.tile([P, PIECE], F32, name="bank")
                nc.tensor.matmul(bank[:], weights[:, expert, rows], picked, start=True, stop=True)
                nc.vector.tensor_tensor(staged[:, half, entries], bank[:], gates[:, entries], mult)
                if expert == 0:
                    nc.scalar.dma_start(out[rows, entries], staged[:, half, entries])
                elif expert == EXPERTS - 1:
                    queue = nc.sync if piece == 0 else nc.scalar
                    queue.dma_start(out[rows, entries], staged[:, half, entries])
                elif piece == PIECES_PER_EXPERT - 1:
                    entries = slice(expert * PER_EXPERT, (expert + 1) * PER_EXPERT)
                    queue = nc.sync if half == 0 else nc.scalar
                    queue.dma_start(out[rows, entries], staged[:, half, entries])
